import numpy as np
import ml_dtypes

BF16 = ml_dtypes.bfloat16


def bf(x):
    return np.asarray(x, np.float32).astype(BF16)


def f32(x):
    return np.asarray(x, np.float32)


def f64(x):
    return np.asarray(x).astype(np.float64)


def striped(idx):
    return np.concatenate([l.reshape(-1, 16).T for l in idx])


def rows(idx, k):
    return np.tile(np.repeat(idx, 16, axis=0), (k // (16 * 8), 1))


def look(tab, idx):
    return np.take_along_axis(f64(tab), rows(idx, len(tab)), axis=1)


K, S, D, V, N = 256, 2048, 3, 1024, 3072


def setup_inputs():
    return {"tab": f32(0.7 * np.random.standard_normal((D, K, S))), "base": f32(np.random.standard_normal((K, V))), "offs": striped(np.random.randint(0, S, (8, N)))}


def reference(tab, base, offs):
    idx = np.stack([g.T.reshape(-1) for g in np.split(offs, 8)])
    x = f64(base) + sum(look(tab[d], idx[:, d * V:(d + 1) * V]) for d in range(D))
    return x

@@ -1,0 +1,41 @@
+import concourse.mybir as mybir
+
+P = 128
+GROUP = 16
+PIECE = 512
+
+F32 = mybir.dt.float32
+U16 = mybir.dt.uint16
+ADD = mybir.AluOpType.add
+
+
+def tile_lookup_res_add_out_kernel(tc, tab, base, offs, out):
+    nc = tc.nc
+    stages, rows, codewords = tab.shape
+    vectors = base.shape[1]
+    blocks, pieces = rows // P, vectors // PIECE
+
+    with tc.tile_pool(name="held", bufs=1) as held:
+        offsets = held.tile([P, stages * vectors // GROUP], U16, name="offsets")
+        nc.sync.dma_start(offsets[:], offs)
+
+        sums, codebooks = {}, {}
+        for b in range(blocks):
+            block_rows = slice(b * P, (b + 1) * P)
+            for c in range(pieces):
+                sums[b, c] = held.tile([P, PIECE], F32, name=f"base_{b}_{c}")
+                nc.sync.dma_start(sums[b, c][:], base[block_rows, c * PIECE:(c + 1) * PIECE])
+            for d in range(stages):
+                codebooks[b, d] = held.tile([P, codewords], F32, name=f"codebook_{b}_{d}")
+                nc.sync.dma_start(codebooks[b, d][:], tab[d, block_rows, :])
+
+        for b in range(blocks):
+            for d in range(stages):
+                for c in range(pieces):
+                    first = (d * vectors + c * PIECE) // GROUP
+                    codes = offsets[:, first:first + PIECE // GROUP]
+                    total = held.tile([P, PIECE], F32, name=f"sum_{b}_{d}_{c}")
+                    nc.vector.tensor_tensor(total[:], codebooks[b, d][:].indirect(codes), sums[b, c][:], ADD)
+                    sums[b, c] = total
+            for c in range(pieces):
+                nc.sync.dma_start(out[b * P:(b + 1) * P, c * PIECE:(c + 1) * PIECE], sums[b, c][:])

@@ -19,23 +19,29 @@ def tile_lookup_res_add_out_kernel(tc, tab, base, offs, out):
         offsets = held.tile([P, stages * vectors // GROUP], U16, name="offsets")
         nc.sync.dma_start(offsets[:], offs)
 
-        sums, codebooks = {}, {}
+        bases, codebooks = {}, {}
         for b in range(blocks):
             block_rows = slice(b * P, (b + 1) * P)
-            for c in range(pieces):
-                sums[b, c] = held.tile([P, PIECE], F32, name=f"base_{b}_{c}")
-                nc.sync.dma_start(sums[b, c][:], base[block_rows, c * PIECE:(c + 1) * PIECE])
+            bases[b] = held.tile([P, vectors], F32, name=f"base_{b}")
+            nc.sync.dma_start(bases[b][:], base[block_rows, :])
             for d in range(stages):
                 codebooks[b, d] = held.tile([P, codewords], F32, name=f"codebook_{b}_{d}")
                 nc.sync.dma_start(codebooks[b, d][:], tab[d, block_rows, :])
 
         for b in range(blocks):
+            block_rows = slice(b * P, (b + 1) * P)
+            running = bases[b]
             for d in range(stages):
+                total = held.tile([P, vectors], F32, name=f"sum_{b}_{d}")
                 for c in range(pieces):
+                    columns = slice(c * PIECE, (c + 1) * PIECE)
                     first = (d * vectors + c * PIECE) // GROUP
                     codes = offsets[:, first:first + PIECE // GROUP]
-                    total = held.tile([P, PIECE], F32, name=f"sum_{b}_{d}_{c}")
-                    nc.vector.tensor_tensor(total[:], codebooks[b, d][:].indirect(codes), sums[b, c][:], ADD)
-                    sums[b, c] = total
-            for c in range(pieces):
-                nc.sync.dma_start(out[b * P:(b + 1) * P, c * PIECE:(c + 1) * PIECE], sums[b, c][:])
+                    nc.vector.tensor_tensor(total[:, columns], codebooks[b, d][:].indirect(codes), running[:, columns], ADD)
+                running = total
+            if b < blocks - 1:
+                nc.sync.dma_start(out[block_rows, :], running[:])
+            else:
+                for c in range(pieces):
+                    columns = slice(c * PIECE, (c + 1) * PIECE)
+                    nc.sync.dma_start(out[block_rows, columns], running[:, columns])

@@ -23,10 +23,13 @@ def tile_lookup_res_add_out_kernel(tc, tab, base, offs, out):
         for b in range(blocks):
             block_rows = slice(b * P, (b + 1) * P)
             bases[b] = held.tile([P, vectors], F32, name=f"base_{b}")
-            nc.sync.dma_start(bases[b][:], base[block_rows, :])
             for d in range(stages):
                 codebooks[b, d] = held.tile([P, codewords], F32, name=f"codebook_{b}_{d}")
                 nc.sync.dma_start(codebooks[b, d][:], tab[d, block_rows, :])
+                if d == 0:
+                    for c in range(pieces):
+                        columns = slice(c * PIECE, (c + 1) * PIECE)
+                        nc.sync.dma_start(bases[b][:, columns], base[block_rows, columns])
 
         for b in range(blocks):
             block_rows = slice(b * P, (b + 1) * P)

import concourse.mybir as mybir

P = 128
GROUP = 16
PIECE = 512

F32 = mybir.dt.float32
U16 = mybir.dt.uint16
ADD = mybir.AluOpType.add


def tile_lookup_res_add_out_kernel(tc, tab, base, offs, out):
    nc = tc.nc
    stages, rows, codewords = tab.shape
    vectors = base.shape[1]
    blocks, pieces = rows // P, vectors // PIECE

    with tc.tile_pool(name="held", bufs=1) as held:
        offsets = held.tile([P, stages * vectors // GROUP], U16, name="offsets")
        nc.sync.dma_start(offsets[:], offs)

        bases, codebooks = {}, {}
        for b in range(blocks):
            block_rows = slice(b * P, (b + 1) * P)
            bases[b] = held.tile([P, vectors], F32, name=f"base_{b}")
            for d in range(stages):
                codebooks[b, d] = held.tile([P, codewords], F32, name=f"codebook_{b}_{d}")
                nc.sync.dma_start(codebooks[b, d][:], tab[d, block_rows, :])
                if d == 0:
                    for c in range(pieces):
                        columns = slice(c * PIECE, (c + 1) * PIECE)
                        nc.sync.dma_start(bases[b][:, columns], base[block_rows, columns])

        for b in range(blocks):
            block_rows = slice(b * P, (b + 1) * P)
            running = bases[b]
            for d in range(stages):
                total = held.tile([P, vectors], F32, name=f"sum_{b}_{d}")
                for c in range(pieces):
                    columns = slice(c * PIECE, (c + 1) * PIECE)
                    first = (d * vectors + c * PIECE) // GROUP
                    codes = offsets[:, first:first + PIECE // GROUP]
                    nc.vector.tensor_tensor(total[:, columns], codebooks[b, d][:].indirect(codes), running[:, columns], ADD)
                running = total
            if b < blocks - 1:
                nc.sync.dma_start(out[block_rows, :], running[:])
            else:
                for c in range(pieces):
                    columns = slice(c * PIECE, (c + 1) * PIECE)
                    nc.sync.dma_start(out[block_rows, columns], running[:, columns])
